import numpy as np
import ml_dtypes


def mxq(x, axis, fmt="e4m3"):
    dtype, down = {"e4m3": (ml_dtypes.float8_e4m3fn, 7), "e5m2": (ml_dtypes.float8_e5m2, 14)}[fmt]
    v = np.moveaxis(np.asarray(x, np.float32).astype(ml_dtypes.bfloat16).astype(np.float64), axis, -1)
    blocks = v.reshape(v.shape[:-1] + (-1, 32))
    amax = np.abs(blocks).max(-1, keepdims=True)
    byte = np.maximum(np.where(amax > 0, np.frexp(amax)[1] - 1 + 127, 0) - down, 1)
    scale = np.exp2(byte - 127.0)
    codes = (blocks / scale).astype(np.float32).astype(dtype).astype(np.float64)
    return np.moveaxis((codes * scale).reshape(v.shape), -1, axis)


WIDE = False


def mx_kscale(k):
    if not WIDE:
        return np.ones(k)
    levels = np.array([10, -10, 5, -5, 0])
    if k % 512:
        return np.exp2(np.random.permutation(np.resize(levels, k // 32))).repeat(32)
    a = np.empty((k // 512, 16))
    for p in range(k // 512):
        a[p, :8] = np.random.permutation(np.resize(levels, 8))
        for g in range(8):
            far = levels[np.abs(levels - a[p, g]) >= 10]
            a[p, g + 8] = far[np.random.randint(len(far))]
    return np.exp2(a.ravel()).repeat(32)


def f64(x):
    return np.asarray(x).astype(np.float64)


def striped(idx):
    return np.tile(idx.reshape(-1, 16).T, (8, 1)).astype(np.uint16)


def unstriped(offs):
    return offs[:16].T.reshape(-1).astype(np.int64)


def striped8(idx):
    return np.concatenate([x.reshape(-1, 16).T for x in idx]).astype(np.uint16)


def runs(offs, k):
    lists = np.stack([offs[16 * r : 16 * r + 16].T.reshape(-1) for r in range(8)]).astype(np.int64)
    return lists[np.arange(k) % 512 // 64]


def pack_weight(w):
    k, n = w.shape
    w = f64(np.asarray(w, np.float32).astype(ml_dtypes.bfloat16)).reshape(k // 32, 32, n)
    amax = np.abs(w).max(1)
    byte = np.clip(np.where(amax > 0, np.frexp(amax)[1] - 1 + 127 - 7, 1), 1, 254)
    scaled = (w * np.exp2(127.0 - byte)[:, None, :]).reshape(k, n).astype(np.float32)
    words = np.ascontiguousarray(scaled.reshape(k // 512, 128, 4, n).transpose(0, 1, 3, 2)).astype(ml_dtypes.float8_e4m3fn).view(np.uint8)
    return words, np.ascontiguousarray(byte.astype(np.uint8).reshape(k // 512, 16, n))


def unpack_weight(words, scales):
    g, p, n, _ = words.shape
    vals = np.ascontiguousarray(words).view(ml_dtypes.float8_e4m3fn).astype(np.float64) * np.repeat(np.exp2(scales.astype(np.float64) - 127.0), 8, axis=1)[..., None]
    return vals.transpose(0, 1, 3, 2).reshape(g * 512, n)


K, T, S, N, H = 512, 2048, 512, 512, 512


def setup_inputs():
    n = np.random.standard_normal
    s = mx_kscale(K)[:, None]
    u = mx_kscale(H)
    packed_xT = pack_weight(n((K, T)) * s)
    return {
        "x_words": packed_xT[0],
        "x_scales": packed_xT[1],
        "w1": (n((K, H)) / np.sqrt(K) / s).astype(np.float32),
        "gn": (np.random.uniform(0.5, 1.5, (H, 1)) * u[:, None]).astype(np.float32),
        "w2": (n((H, N)) / np.sqrt(2 * H) / u[:, None]).astype(np.float32),
        "w3": (n((K, N)) / np.sqrt(2 * K) / s).astype(np.float32),
        "offs": striped8(np.random.randint(0, T, (8, S))),
        "n1": striped8(np.stack([np.random.permutation(S) for _ in range(8)])),
        "n2": striped8(np.stack([np.random.permutation(S) for _ in range(8)])),
        "two": striped(np.random.permutation(T)[:S]),
        "n3": striped(np.random.permutation(S)),
        "n4": striped(np.random.permutation(S)),
    }


def reference(x_words, x_scales, w1, gn, w2, w3, offs, n1, n2, two, n3, n4):
    xq = unpack_weight(x_words, x_scales)[np.arange(K)[:, None], runs(offs, K)]
    y = mxq(f64(w1), 0, "e4m3").T @ xq
    z = f64(gn) * (0.75 * (y[np.arange(H)[:, None], runs(n1, H)] + y[np.arange(H)[:, None], runs(n2, H)]) - y)
    x_two = unpack_weight(x_words, x_scales)[:, unstriped(two)]
    h = mxq(f64(w2), 0, "e4m3").T @ mxq(z, 0, "e4m3") + mxq(f64(w3), 0, "e4m3").T @ x_two
    st = h - h[:, unstriped(n3)]
    return st / (np.abs(st[:, unstriped(n4)]) + 0.5)

@@ -1,0 +1,195 @@
+from contextlib import ExitStack
+
+import concourse.mybir as mybir
+
+K, T, S, H, N = 512, 2048, 512, 512, 512
+FLOPS = 2 * S * (K * H + H * N + K * N)
+
+F32 = mybir.dt.float32
+BF16 = mybir.dt.bfloat16
+I32 = mybir.dt.int32
+U32 = mybir.dt.uint32
+U16 = mybir.dt.uint16
+U8 = mybir.dt.uint8
+FP8X4 = mybir.dt.float8_e4m3fn_x4
+ALU = mybir.AluOpType
+ACT = mybir.ActivationFunctionType
+
+P = 128
+PACK = 4
+LIST_ROWS = 16
+SPARE = 16
+PIECES = ((0, 256), (256, 384), (384, 512))
+
+
+def tile_picked_hmixlaphopn_none_p_kernel(tc, x_words, x_scales, w1, gn, w2, w3, offs, n1, n2, two, n3, n4, out):
+    nc = tc.nc
+    with ExitStack() as ctx:
+        lists = ctx.enter_context(tc.tile_pool(name="lists", bufs=1))
+        keep = ctx.enter_context(tc.tile_pool(name="keep", bufs=1))
+        psum = ctx.enter_context(tc.psum_pool(name="psum", bufs=1))
+
+        def load_list(name, source):
+            tile = lists.tile([P, S // LIST_ROWS], U16, name=name)
+            nc.sync.dma_start(tile[:], source)
+            return tile
+
+        def entries(list_tile, first, last):
+            return list_tile[:, first // LIST_ROWS : last // LIST_ROWS]
+
+        def quantise(name, rounded, width):
+            codes = keep.tile([P, width], U32, name=name + "_codes", align_bytes=64)
+            scales = keep.tile([P, width], U8, name=name + "_scales", align_bytes=64)
+            nc.vector.quantize_mx(out=codes[:].bitcast(FP8X4), scales=scales[:], in_=rounded)
+            return codes, scales
+
+        table_scales = keep.tile([P, T], U8, name="table_scales", tag="scales_then_weights")
+        nc.gpsimd.memset(table_scales[:].bitcast(I32), 0)
+        scale_rows = x_scales[0].bitcast(I32)
+
+        offs_list = load_list("offs_list", offs)
+        w1_raw = [keep.tile([P, PACK, H // 2], F32, name="w1_raw%d" % half) for half in range(2)]
+        w1_rows = w1.rearrange("(p j) c -> p j c", j=PACK)
+        nc.sync.dma_start(w1_raw[0][:], w1_rows[:, :, : H // 2])
+        for r in (0, 1):
+            nc.sync.dma_start(table_scales[r:P:16, :].bitcast(I32), scale_rows[r:16:2, :])
+        for r in (2, 3):
+            nc.sync.dma_start(table_scales[r:P:32, :].bitcast(I32), scale_rows[r:16:4, :])
+        table_words = keep.tile([P, T], U32, name="table_words")
+        nc.sync.dma_start(table_words[:].bitcast(I32), x_words[0].rearrange("p n t -> p (n t)").bitcast(I32))
+        nc.sync.dma_start(w1_raw[1][:], w1_rows[:, :, H // 2 :])
+        two_list = load_list("two_list", two)
+        gain = keep.tile([P, PACK], F32, name="gain")
+        nc.sync.dma_start(gain[:], gn.rearrange("(p t) o -> p (t o)", t=PACK))
+        n1_list = load_list("n1_list", n1)
+        n2_list = load_list("n2_list", n2)
+        n3_list = load_list("n3_list", n3)
+        n4_list = load_list("n4_list", n4)
+
+        h_rows, root_rows = [], []
+        for m in range(N // P):
+            for name, group in (("h", h_rows), ("root", root_rows)):
+                tile = keep.tile([P, S + SPARE], F32, name="%s_rows%d" % (name, m))
+                nc.gpsimd.memset(tile[:, S:], 0.0)
+                group.append(tile)
+
+        picked_bytes = keep.tile([P, S], U8, name="picked_bytes")
+        nc.vector.tensor_copy(picked_bytes[:], table_scales[:].indirect(offs_list[:]))
+        x_plane = keep.tile([P, S], U8, name="x_plane", align_bytes=64)
+        nc.vector.tensor_copy(x_plane[:].bitcast(I32), picked_bytes[:].bitcast(I32))
+        for r in (0, 1):
+            nc.scalar.dma_start(x_plane[2 + r : P : 32, :].bitcast(I32), picked_bytes[16 + r : P : 32, :].bitcast(I32))
+        two_plane = keep.tile([P, S], U8, name="two_plane", align_bytes=64)
+        nc.vector.tensor_copy(two_plane[:], table_scales[:].indirect(two_list[:]))
+        later_weights = keep.tile([P, 2, PACK, N], F32, name="later_weights", tag="scales_then_weights")
+        for slot, source in enumerate((w3, w2)):
+            nc.sync.dma_start(later_weights[:, slot], source.rearrange("(p j) c -> p j c", j=PACK))
+        x_codes = keep.tile([P, S], U32, name="x_codes", align_bytes=64)
+        nc.vector.tensor_copy(x_codes[:], table_words[:].indirect(offs_list[:]))
+
+        w1_rounded = keep.tile([P, PACK, P * PACK], BF16, name="w1_rounded", align_bytes=64)
+        for half, copy in enumerate((nc.scalar.copy, nc.vector.tensor_copy)):
+            copy(
+                w1_rounded[:].rearrange("p t (m j) -> p m j t", j=PACK)[:, half * P // 2 : (half + 1) * P // 2],
+                w1_raw[half][:].rearrange("p j (m t) -> p m j t", t=PACK),
+            )
+        y_banks, y_rows = [], []
+        for t in range(PACK):
+            codes, scales = quantise("w1_%d" % t, w1_rounded[:, t, :], P)
+            bank = psum.tile([P, S], F32, name="y_bank%d" % t)
+            nc.tensor.matmul_mx(
+                out=bank[:], lhsT=codes[:].bitcast(FP8X4), lhsT_scale=scales[:],
+                rhs=x_codes[:].bitcast(FP8X4), rhs_scale=x_plane[:], start=True, stop=True,
+            )
+            y_banks.append(bank)
+        for t in range(PACK):
+            rows = keep.tile([P, S], F32, name="y_rows%d" % t)
+            nc.vector.tensor_scalar(rows[:], y_banks[t][:], gain[:, t : t + 1], 0.75, ALU.mult, ALU.mult)
+            y_rows.append(rows)
+
+        two_codes = keep.tile([P, S], U32, name="two_codes", align_bytes=64)
+        nc.vector.tensor_copy(two_codes[:], table_words[:].indirect(two_list[:]))
+
+        def prepare_weight(name, raw):
+            rounded = keep.tile([P, N * PACK], BF16, name=name + "_rounded", tag=name + "_then_rest", align_bytes=64)
+            nc.vector.tensor_copy(
+                rounded[:].rearrange("p (c i j) -> p c j i", i=4, j=PACK),
+                raw.rearrange("p j (c i) -> p c j i", i=4),
+            )
+            return quantise(name, rounded[:], N)
+
+        h_banks = [psum.tile([P, S], F32, name="h_bank%d" % m) for m in range(N // P)]
+
+        def second_product_pass(weight, moving_codes, moving_scales, blocks, first, last, start, stop):
+            for m in blocks:
+                block = slice(m * P, (m + 1) * P)
+                nc.tensor.matmul_mx(
+                    out=h_banks[m][:, first:last], lhsT=weight[0][:, block].bitcast(FP8X4), lhsT_scale=weight[1][:, block],
+                    rhs=moving_codes.bitcast(FP8X4), rhs_scale=moving_scales, start=start, stop=stop,
+                )
+
+        def hidden_piece(first, last, tag):
+            width = last - first
+            near1 = keep.tile([P, PACK, width], F32, name="near1_%d" % first)
+            near2 = keep.tile([P, PACK, width], F32, name="near2_%d" % first)
+            rest = keep.tile([P, PACK, width], F32, name="rest_%d" % first, tag=tag, align_bytes=64)
+            for t in range(PACK):
+                nc.scalar.activation(near1[:, t, :], y_rows[t][:].indirect(entries(n1_list, first, last)), ACT.Copy)
+                nc.scalar.activation(near2[:, t, :], y_rows[t][:].indirect(entries(n2_list, first, last)), ACT.Copy)
+                nc.vector.scalar_tensor_tensor(
+                    rest[:, t, :], y_banks[t][:, first:last], gain[:, t : t + 1], near1[:, t, :], ALU.mult, ALU.subtract
+                )
+            z_rounded = keep.tile([P, width * PACK], BF16, name="z_rounded%d" % first, align_bytes=64)
+            nc.vector.tensor_tensor(
+                z_rounded[:].rearrange("p (c i t) -> p c t i", i=4, t=PACK),
+                near2[:].rearrange("p t (c i) -> p c t i", i=4),
+                rest[:].rearrange("p t (c i) -> p c t i", i=4),
+                ALU.subtract,
+            )
+            return quantise("z_%d" % first, z_rounded[:], width)
+
+        w3_q = prepare_weight("w3", later_weights[:, 0])
+        second_product_pass(w3_q, two_codes[:], two_plane[:], range(1, N // P), 0, S, True, False)
+        w2_q = None
+        for (first, last), tag in zip(PIECES, ("w3_then_rest", "w2_then_rest", "rest")):
+            z_codes, z_scales = hidden_piece(first, last, tag)
+            if w2_q is None:
+                w2_q = prepare_weight("w2", later_weights[:, 1])
+            second_product_pass(w3_q, two_codes[:, first:last], two_plane[:, first:last], [0], first, last, True, False)
+            second_product_pass(w2_q, z_codes[:], z_scales[:], [0], first, last, False, True)
+            copy = nc.scalar.copy if last == S else nc.vector.tensor_copy
+            copy(h_rows[0][:, first:last], h_banks[0][:, first:last])
+            second_product_pass(w2_q, z_codes[:], z_scales[:], range(1, N // P), first, last, False, last == S)
+
+        st_rows = []
+
+        def difference(m):
+            if m > 0:
+                nc.vector.tensor_copy(h_rows[m][:, :S], h_banks[m][:])
+            other = keep.tile([P, S], F32, name="other%d" % m)
+            nc.scalar.activation(other[:], h_rows[m][:].indirect(n3_list[:]), ACT.Copy)
+            st = keep.tile([P, S], F32, name="st%d" % m)
+            nc.vector.tensor_tensor(st[:], h_banks[m][:], other[:], ALU.subtract)
+            size = keep.tile([P, S], F32, name="size%d" % m)
+            nc.vector.scalar_tensor_tensor(size[:], st[:], -1.0, st[:], ALU.mult, ALU.max)
+            st_rows.append((st, size))
+
+        def normalise(m):
+            st, size = st_rows[m]
+            nc.scalar.activation(root_rows[m][:, :S], size[:], ACT.Abs_reciprocal_sqrt, bias=0.5)
+            cuts = (0, 256, 384, S) if m == N // P - 1 else (0, S)
+            for first, last in zip(cuts, cuts[1:]):
+                width = last - first
+                root = keep.tile([P, width], F32, name="root%d_%d" % (m, first))
+                nc.scalar.activation(root[:], root_rows[m][:].indirect(entries(n4_list, first, last)), ACT.Copy)
+                half = keep.tile([P, width], F32, name="half%d_%d" % (m, first))
+                nc.vector.tensor_tensor(half[:], st[:, first:last], root[:], ALU.mult)
+                result = keep.tile([P, width], F32, name="result%d_%d" % (m, first))
+                nc.vector.tensor_tensor(result[:], half[:], root[:], ALU.mult)
+                nc.sync.dma_start(out[m * P : (m + 1) * P, first:last], result[:])
+
+        difference(0)
+        for m in range(1, N // P):
+            difference(m)
+            normalise(m - 1)
+        normalise(N // P - 1)

@@ -48,6 +48,7 @@ def tile_picked_hmixlaphopn_none_p_kernel(tc, x_words, x_scales, w1, gn, w2, w3,
         scale_rows = x_scales[0].bitcast(I32)
 
         offs_list = load_list("offs_list", offs)
+        two_list = load_list("two_list", two)
         w1_raw = [keep.tile([P, PACK, H // 2], F32, name="w1_raw%d" % half) for half in range(2)]
         w1_rows = w1.rearrange("(p j) c -> p j c", j=PACK)
         nc.sync.dma_start(w1_raw[0][:], w1_rows[:, :, : H // 2])
@@ -58,9 +59,8 @@ def tile_picked_hmixlaphopn_none_p_kernel(tc, x_words, x_scales, w1, gn, w2, w3,
         table_words = keep.tile([P, T], U32, name="table_words")
         nc.sync.dma_start(table_words[:].bitcast(I32), x_words[0].rearrange("p n t -> p (n t)").bitcast(I32))
         nc.sync.dma_start(w1_raw[1][:], w1_rows[:, :, H // 2 :])
-        two_list = load_list("two_list", two)
         gain = keep.tile([P, PACK], F32, name="gain")
-        nc.sync.dma_start(gain[:], gn.rearrange("(p t) o -> p (t o)", t=PACK))
+        nc.gpsimd.dma_start(gain[:], gn.rearrange("(p t) o -> p (t o)", t=PACK))
         n1_list = load_list("n1_list", n1)
         n2_list = load_list("n2_list", n2)
         n3_list = load_list("n3_list", n3)
@@ -73,13 +73,18 @@ def tile_picked_hmixlaphopn_none_p_kernel(tc, x_words, x_scales, w1, gn, w2, w3,
                 nc.gpsimd.memset(tile[:, S:], 0.0)
                 group.append(tile)
 
-        picked_bytes = keep.tile([P, S], U8, name="picked_bytes")
+        warm = keep.tile([P, 1], F32, name="warm")
+        nc.scalar.activation(warm[:], h_rows[0][:, S : S + 1], ACT.Abs_reciprocal_sqrt, bias=0.5)
+        near_gain = keep.tile([P, PACK], F32, name="near_gain")
+        nc.gpsimd.tensor_scalar(near_gain[:], gain[:], 0.75, 0.0, ALU.mult, ALU.add)
+
+        picked_bytes = keep.tile([P, S], U8, name="picked_bytes", tag="picked_then_two", align_bytes=64)
         nc.vector.tensor_copy(picked_bytes[:], table_scales[:].indirect(offs_list[:]))
         x_plane = keep.tile([P, S], U8, name="x_plane", align_bytes=64)
         nc.vector.tensor_copy(x_plane[:].bitcast(I32), picked_bytes[:].bitcast(I32))
         for r in (0, 1):
-            nc.scalar.dma_start(x_plane[2 + r : P : 32, :].bitcast(I32), picked_bytes[16 + r : P : 32, :].bitcast(I32))
-        two_plane = keep.tile([P, S], U8, name="two_plane", align_bytes=64)
+            nc.scalar.dma_start(x_plane[2 + r : P : 32, :].bitcast(I32), x_plane[16 + r : P : 32, :].bitcast(I32))
+        two_plane = keep.tile([P, S], U8, name="two_plane", tag="picked_then_two", align_bytes=64)
         nc.vector.tensor_copy(two_plane[:], table_scales[:].indirect(two_list[:]))
         later_weights = keep.tile([P, 2, PACK, N], F32, name="later_weights", tag="scales_then_weights")
         for slot, source in enumerate((w3, w2)):
@@ -87,11 +92,14 @@ def tile_picked_hmixlaphopn_none_p_kernel(tc, x_words, x_scales, w1, gn, w2, w3,
         x_codes = keep.tile([P, S], U32, name="x_codes", align_bytes=64)
         nc.vector.tensor_copy(x_codes[:], table_words[:].indirect(offs_list[:]))
 
-        w1_rounded = keep.tile([P, PACK, P * PACK], BF16, name="w1_rounded", align_bytes=64)
-        for half, copy in enumerate((nc.scalar.copy, nc.vector.tensor_copy)):
+        w1_rounded = keep.tile([P, PACK, P * PACK], BF16, name="w1_rounded", tag="w1_then_two", align_bytes=64)
+        dealt = w1_rounded[:].rearrange("p t (m j) -> p m j t", j=PACK)
+        for half, first, last, copy in (
+            (0, 0, 64, nc.scalar.copy), (1, 0, 24, nc.scalar.copy), (1, 24, 64, nc.vector.tensor_copy)
+        ):
             copy(
-                w1_rounded[:].rearrange("p t (m j) -> p m j t", j=PACK)[:, half * P // 2 : (half + 1) * P // 2],
-                w1_raw[half][:].rearrange("p j (m t) -> p m j t", t=PACK),
+                dealt[:, half * 64 + first : half * 64 + last],
+                w1_raw[half][:].rearrange("p j (m t) -> p m j t", t=PACK)[:, first:last],
             )
         y_banks, y_rows = [], []
         for t in range(PACK):
@@ -104,18 +112,23 @@ def tile_picked_hmixlaphopn_none_p_kernel(tc, x_words, x_scales, w1, gn, w2, w3,
             y_banks.append(bank)
         for t in range(PACK):
             rows = keep.tile([P, S], F32, name="y_rows%d" % t)
-            nc.vector.tensor_scalar(rows[:], y_banks[t][:], gain[:, t : t + 1], 0.75, ALU.mult, ALU.mult)
+            if t == 0:
+                nc.scalar.activation(rows[:], y_banks[t][:], ACT.Copy, scale=near_gain[:, t : t + 1])
+            else:
+                nc.vector.tensor_scalar(rows[:], y_banks[t][:], gain[:, t : t + 1], 0.75, ALU.mult, ALU.mult)
             y_rows.append(rows)
 
-        two_codes = keep.tile([P, S], U32, name="two_codes", align_bytes=64)
+        two_codes = keep.tile([P, S], U32, name="two_codes", tag="w1_then_two", align_bytes=64)
         nc.vector.tensor_copy(two_codes[:], table_words[:].indirect(two_list[:]))
 
         def prepare_weight(name, raw):
             rounded = keep.tile([P, N * PACK], BF16, name=name + "_rounded", tag=name + "_then_rest", align_bytes=64)
-            nc.vector.tensor_copy(
-                rounded[:].rearrange("p (c i j) -> p c j i", i=4, j=PACK),
-                raw.rearrange("p j (c i) -> p c j i", i=4),
-            )
+            for m in range(N // P):
+                nc.gpsimd.tensor_scalar(
+                    rounded[:, m * P * PACK : (m + 1) * P * PACK].rearrange("p (c j) -> p c j", j=PACK),
+                    raw[:, :, m * P : (m + 1) * P].rearrange("p j c -> p c j"),
+                    1.0, 0.0, ALU.mult, ALU.add,
+                )
             return quantise(name, rounded[:], N)
 
         h_banks = [psum.tile([P, S], F32, name="h_bank%d" % m) for m in range(N // P)]
@@ -132,14 +145,14 @@ def tile_picked_hmixlaphopn_none_p_kernel(tc, x_words, x_scales, w1, gn, w2, w3,
             width = last - first
             near1 = keep.tile([P, PACK, width], F32, name="near1_%d" % first)
             near2 = keep.tile([P, PACK, width], F32, name="near2_%d" % first)
-            rest = keep.tile([P, PACK, width], F32, name="rest_%d" % first, tag=tag, align_bytes=64)
+            rest = keep.tile([P, PACK, width], F32, name="rest_%d" % first)
             for t in range(PACK):
                 nc.scalar.activation(near1[:, t, :], y_rows[t][:].indirect(entries(n1_list, first, last)), ACT.Copy)
                 nc.scalar.activation(near2[:, t, :], y_rows[t][:].indirect(entries(n2_list, first, last)), ACT.Copy)
                 nc.vector.scalar_tensor_tensor(
                     rest[:, t, :], y_banks[t][:, first:last], gain[:, t : t + 1], near1[:, t, :], ALU.mult, ALU.subtract
                 )
-            z_rounded = keep.tile([P, width * PACK], BF16, name="z_rounded%d" % first, align_bytes=64)
+            z_rounded = keep.tile([P, width * PACK], BF16, name="z_rounded%d" % first, tag=tag, align_bytes=64)
             nc.vector.tensor_tensor(
                 z_rounded[:].rearrange("p (c i t) -> p c t i", i=4, t=PACK),
                 near2[:].rearrange("p t (c i) -> p c t i", i=4),
@@ -151,7 +164,7 @@ def tile_picked_hmixlaphopn_none_p_kernel(tc, x_words, x_scales, w1, gn, w2, w3,
         w3_q = prepare_weight("w3", later_weights[:, 0])
         second_product_pass(w3_q, two_codes[:], two_plane[:], range(1, N // P), 0, S, True, False)
         w2_q = None
-        for (first, last), tag in zip(PIECES, ("w3_then_rest", "w2_then_rest", "rest")):
+        for (first, last), tag in zip(PIECES, ("w3_then_rest", "w2_then_rest", "z")):
             z_codes, z_scales = hidden_piece(first, last, tag)
             if w2_q is None:
                 w2_q = prepare_weight("w2", later_weights[:, 1])
@@ -171,21 +184,24 @@ def tile_picked_hmixlaphopn_none_p_kernel(tc, x_words, x_scales, w1, gn, w2, w3,
             st = keep.tile([P, S], F32, name="st%d" % m)
             nc.vector.tensor_tensor(st[:], h_banks[m][:], other[:], ALU.subtract)
             size = keep.tile([P, S], F32, name="size%d" % m)
-            nc.vector.scalar_tensor_tensor(size[:], st[:], -1.0, st[:], ALU.mult, ALU.max)
+            nc.vector.tensor_reduce(
+                size[:], st[:].rearrange("p (c o) -> p c o", o=1), mybir.AxisListType.X, ALU.max, apply_absolute_value=True
+            )
             st_rows.append((st, size))
 
         def normalise(m):
             st, size = st_rows[m]
             nc.scalar.activation(root_rows[m][:, :S], size[:], ACT.Abs_reciprocal_sqrt, bias=0.5)
             cuts = (0, 256, 384, S) if m == N // P - 1 else (0, S)
+            engine = nc.vector
             for first, last in zip(cuts, cuts[1:]):
                 width = last - first
                 root = keep.tile([P, width], F32, name="root%d_%d" % (m, first))
                 nc.scalar.activation(root[:], root_rows[m][:].indirect(entries(n4_list, first, last)), ACT.Copy)
                 half = keep.tile([P, width], F32, name="half%d_%d" % (m, first))
-                nc.vector.tensor_tensor(half[:], st[:, first:last], root[:], ALU.mult)
+                engine.tensor_tensor(half[:], st[:, first:last], root[:], ALU.mult)
                 result = keep.tile([P, width], F32, name="result%d_%d" % (m, first))
-                nc.vector.tensor_tensor(result[:], half[:], root[:], ALU.mult)
+                engine.tensor_tensor(result[:], half[:], root[:], ALU.mult)
                 nc.sync.dma_start(out[m * P : (m + 1) * P, first:last], result[:])
 
         difference(0)

@@ -38,7 +38,7 @@ def tile_picked_hmixlaphopn_none_p_kernel(tc, x_words, x_scales, w1, gn, w2, w3,
             return list_tile[:, first // LIST_ROWS : last // LIST_ROWS]
 
         def quantise(name, rounded, width):
-            codes = keep.tile([P, width], U32, name=name + "_codes", align_bytes=64)
+            codes = keep.tile([P, width], U32, name=name + "_codes", tag=name + "_codes", align_bytes=64)
             scales = keep.tile([P, width], U8, name=name + "_scales", align_bytes=64)
             nc.vector.quantize_mx(out=codes[:].bitcast(FP8X4), scales=scales[:], in_=rounded)
             return codes, scales
@@ -51,13 +51,15 @@ def tile_picked_hmixlaphopn_none_p_kernel(tc, x_words, x_scales, w1, gn, w2, w3,
         two_list = load_list("two_list", two)
         w1_raw = [keep.tile([P, PACK, H // 2], F32, name="w1_raw%d" % half) for half in range(2)]
         w1_rows = w1.rearrange("(p j) c -> p j c", j=PACK)
-        nc.sync.dma_start(w1_raw[0][:], w1_rows[:, :, : H // 2])
+        table_words = keep.tile([P, T], U32, name="table_words")
+        word_rows = x_words[0].rearrange("p n t -> p (n t)").bitcast(I32)
+        nc.sync.dma_start(table_words[:, : T // 4].bitcast(I32), word_rows[:, : T // 4])
         for r in (0, 1):
             nc.sync.dma_start(table_scales[r:P:16, :].bitcast(I32), scale_rows[r:16:2, :])
         for r in (2, 3):
             nc.sync.dma_start(table_scales[r:P:32, :].bitcast(I32), scale_rows[r:16:4, :])
-        table_words = keep.tile([P, T], U32, name="table_words")
-        nc.sync.dma_start(table_words[:].bitcast(I32), x_words[0].rearrange("p n t -> p (n t)").bitcast(I32))
+        nc.sync.dma_start(table_words[:, T // 4 :].bitcast(I32), word_rows[:, T // 4 :])
+        nc.sync.dma_start(w1_raw[0][:], w1_rows[:, :, : H // 2])
         nc.sync.dma_start(w1_raw[1][:], w1_rows[:, :, H // 2 :])
         gain = keep.tile([P, PACK], F32, name="gain")
         nc.gpsimd.dma_start(gain[:], gn.rearrange("(p t) o -> p (t o)", t=PACK))
@@ -84,13 +86,14 @@ def tile_picked_hmixlaphopn_none_p_kernel(tc, x_words, x_scales, w1, gn, w2, w3,
         nc.vector.tensor_copy(x_plane[:].bitcast(I32), picked_bytes[:].bitcast(I32))
         for r in (0, 1):
             nc.scalar.dma_start(x_plane[2 + r : P : 32, :].bitcast(I32), x_plane[16 + r : P : 32, :].bitcast(I32))
-        two_plane = keep.tile([P, S], U8, name="two_plane", tag="picked_then_two", align_bytes=64)
-        nc.vector.tensor_copy(two_plane[:], table_scales[:].indirect(two_list[:]))
         later_weights = keep.tile([P, 2, PACK, N], F32, name="later_weights", tag="scales_then_weights")
         for slot, source in enumerate((w3, w2)):
             nc.sync.dma_start(later_weights[:, slot], source.rearrange("(p j) c -> p j c", j=PACK))
         x_codes = keep.tile([P, S], U32, name="x_codes", align_bytes=64)
         nc.vector.tensor_copy(x_codes[:], table_words[:].indirect(offs_list[:]))
+
+        two_plane = keep.tile([P, S], U8, name="two_plane", tag="picked_then_two", align_bytes=64)
+        nc.vector.tensor_copy(two_plane[:], table_scales[:].indirect(two_list[:]))
 
         w1_rounded = keep.tile([P, PACK, P * PACK], BF16, name="w1_rounded", tag="w1_then_two", align_bytes=64)
         dealt = w1_rounded[:].rearrange("p t (m j) -> p m j t", j=PACK)
@@ -112,7 +115,7 @@ def tile_picked_hmixlaphopn_none_p_kernel(tc, x_words, x_scales, w1, gn, w2, w3,
             y_banks.append(bank)
         for t in range(PACK):
             rows = keep.tile([P, S], F32, name="y_rows%d" % t)
-            if t == 0:
+            if t % 2 == 0:
                 nc.scalar.activation(rows[:], y_banks[t][:], ACT.Copy, scale=near_gain[:, t : t + 1])
             else:
                 nc.vector.tensor_scalar(rows[:], y_banks[t][:], gain[:, t : t + 1], 0.75, ALU.mult, ALU.mult)
@@ -123,12 +126,10 @@ def tile_picked_hmixlaphopn_none_p_kernel(tc, x_words, x_scales, w1, gn, w2, w3,
 
         def prepare_weight(name, raw):
             rounded = keep.tile([P, N * PACK], BF16, name=name + "_rounded", tag=name + "_then_rest", align_bytes=64)
-            for m in range(N // P):
-                nc.gpsimd.tensor_scalar(
-                    rounded[:, m * P * PACK : (m + 1) * P * PACK].rearrange("p (c j) -> p c j", j=PACK),
-                    raw[:, :, m * P : (m + 1) * P].rearrange("p j c -> p c j"),
-                    1.0, 0.0, ALU.mult, ALU.add,
-                )
+            nc.vector.tensor_copy(
+                rounded[:].rearrange("p (c i j) -> p c j i", i=4, j=PACK),
+                raw.rearrange("p j (c i) -> p c j i", i=4),
+            )
             return quantise(name, rounded[:], N)
 
         h_banks = [psum.tile([P, S], F32, name="h_bank%d" % m) for m in range(N // P)]
@@ -145,7 +146,7 @@ def tile_picked_hmixlaphopn_none_p_kernel(tc, x_words, x_scales, w1, gn, w2, w3,
             width = last - first
             near1 = keep.tile([P, PACK, width], F32, name="near1_%d" % first)
             near2 = keep.tile([P, PACK, width], F32, name="near2_%d" % first)
-            rest = keep.tile([P, PACK, width], F32, name="rest_%d" % first)
+            rest = keep.tile([P, PACK, width], F32, name="rest_%d" % first, tag="w2_then_rest", align_bytes=64)
             for t in range(PACK):
                 nc.scalar.activation(near1[:, t, :], y_rows[t][:].indirect(entries(n1_list, first, last)), ACT.Copy)
                 nc.scalar.activation(near2[:, t, :], y_rows[t][:].indirect(entries(n2_list, first, last)), ACT.Copy)
@@ -163,11 +164,9 @@ def tile_picked_hmixlaphopn_none_p_kernel(tc, x_words, x_scales, w1, gn, w2, w3,
 
         w3_q = prepare_weight("w3", later_weights[:, 0])
         second_product_pass(w3_q, two_codes[:], two_plane[:], range(1, N // P), 0, S, True, False)
-        w2_q = None
-        for (first, last), tag in zip(PIECES, ("w3_then_rest", "w2_then_rest", "z")):
+        w2_q = prepare_weight("w2", later_weights[:, 1])
+        for (first, last), tag in zip(PIECES, ("z0", "z1", "z2")):
             z_codes, z_scales = hidden_piece(first, last, tag)
-            if w2_q is None:
-                w2_q = prepare_weight("w2", later_weights[:, 1])
             second_product_pass(w3_q, two_codes[:, first:last], two_plane[:, first:last], [0], first, last, True, False)
             second_product_pass(w2_q, z_codes[:], z_scales[:], [0], first, last, False, True)
             copy = nc.scalar.copy if last == S else nc.vector.tensor_copy
@@ -184,9 +183,7 @@ def tile_picked_hmixlaphopn_none_p_kernel(tc, x_words, x_scales, w1, gn, w2, w3,
             st = keep.tile([P, S], F32, name="st%d" % m)
             nc.vector.tensor_tensor(st[:], h_banks[m][:], other[:], ALU.subtract)
             size = keep.tile([P, S], F32, name="size%d" % m)
-            nc.vector.tensor_reduce(
-                size[:], st[:].rearrange("p (c o) -> p c o", o=1), mybir.AxisListType.X, ALU.max, apply_absolute_value=True
-            )
+            nc.vector.scalar_tensor_tensor(size[:], st[:], -1.0, st[:], ALU.mult, ALU.max)
             st_rows.append((st, size))
 
         def normalise(m):

@@ -17,9 +17,15 @@ ACT = mybir.ActivationFunctionType
 
 P = 128
 PACK = 4
-LIST_ROWS = 16
+GROUP = 16
+QUADRANT = 32
+SCALE_ROWS = K // 32
+LINE = 4
+BLOCKS = N // P
+HALF = S // 2
 SPARE = 16
-PIECES = ((0, 256), (256, 384), (384, 512))
+PIECES = ((0, HALF), (HALF, HALF + P), (HALF + P, S))
+W1_SCALAR_SHARE = 24
 
 
 def tile_picked_hmixlaphopn_none_p_kernel(tc, x_words, x_scales, w1, gn, w2, w3, offs, n1, n2, two, n3, n4, out):
@@ -30,18 +36,18 @@ def tile_picked_hmixlaphopn_none_p_kernel(tc, x_words, x_scales, w1, gn, w2, w3,
         psum = ctx.enter_context(tc.psum_pool(name="psum", bufs=1))
 
         def load_list(name, source):
-            tile = lists.tile([P, S // LIST_ROWS], U16, name=name)
+            tile = lists.tile([P, S // GROUP], U16, name=name)
             nc.sync.dma_start(tile[:], source)
             return tile
 
         def entries(list_tile, first, last):
-            return list_tile[:, first // LIST_ROWS : last // LIST_ROWS]
+            return list_tile[:, first // GROUP : last // GROUP]
 
         def quantise(name, rounded, width):
-            codes = keep.tile([P, width], U32, name=name + "_codes", tag=name + "_codes", align_bytes=64)
-            scales = keep.tile([P, width], U8, name=name + "_scales", align_bytes=64)
-            nc.vector.quantize_mx(out=codes[:].bitcast(FP8X4), scales=scales[:], in_=rounded)
-            return codes, scales
+            codes = keep.tile([P, width], U32, name=name + "_codes", align_bytes=64)
+            plane = keep.tile([P, width], U8, name=name + "_plane", align_bytes=64)
+            nc.vector.quantize_mx(out=codes[:].bitcast(FP8X4), scales=plane[:], in_=rounded)
+            return codes, plane
 
         table_scales = keep.tile([P, T], U8, name="table_scales", tag="scales_then_weights")
         nc.gpsimd.memset(table_scales[:].bitcast(I32), 0)
@@ -49,18 +55,18 @@ def tile_picked_hmixlaphopn_none_p_kernel(tc, x_words, x_scales, w1, gn, w2, w3,
 
         offs_list = load_list("offs_list", offs)
         two_list = load_list("two_list", two)
-        w1_raw = [keep.tile([P, PACK, H // 2], F32, name="w1_raw%d" % half) for half in range(2)]
-        w1_rows = w1.rearrange("(p j) c -> p j c", j=PACK)
         table_words = keep.tile([P, T], U32, name="table_words")
         word_rows = x_words[0].rearrange("p n t -> p (n t)").bitcast(I32)
         nc.sync.dma_start(table_words[:, : T // 4].bitcast(I32), word_rows[:, : T // 4])
         for r in (0, 1):
-            nc.sync.dma_start(table_scales[r:P:16, :].bitcast(I32), scale_rows[r:16:2, :])
+            nc.sync.dma_start(table_scales[r:P:GROUP, :].bitcast(I32), scale_rows[r:SCALE_ROWS:2, :])
         for r in (2, 3):
-            nc.sync.dma_start(table_scales[r:P:32, :].bitcast(I32), scale_rows[r:16:4, :])
+            nc.sync.dma_start(table_scales[r:P:QUADRANT, :].bitcast(I32), scale_rows[r:SCALE_ROWS:4, :])
         nc.sync.dma_start(table_words[:, T // 4 :].bitcast(I32), word_rows[:, T // 4 :])
-        nc.sync.dma_start(w1_raw[0][:], w1_rows[:, :, : H // 2])
-        nc.sync.dma_start(w1_raw[1][:], w1_rows[:, :, H // 2 :])
+        w1_rows = w1.rearrange("(p j) c -> p j c", j=PACK)
+        w1_raw = [keep.tile([P, PACK, H // 2], F32, name="w1_raw%d" % half) for half in range(2)]
+        for half in range(2):
+            nc.sync.dma_start(w1_raw[half][:], w1_rows[:, :, half * H // 2 : (half + 1) * H // 2])
         gain = keep.tile([P, PACK], F32, name="gain")
         nc.gpsimd.dma_start(gain[:], gn.rearrange("(p t) o -> p (t o)", t=PACK))
         n1_list = load_list("n1_list", n1)
@@ -69,14 +75,14 @@ def tile_picked_hmixlaphopn_none_p_kernel(tc, x_words, x_scales, w1, gn, w2, w3,
         n4_list = load_list("n4_list", n4)
 
         h_rows, root_rows = [], []
-        for m in range(N // P):
-            for name, group in (("h", h_rows), ("root", root_rows)):
-                tile = keep.tile([P, S + SPARE], F32, name="%s_rows%d" % (name, m))
-                nc.gpsimd.memset(tile[:, S:], 0.0)
-                group.append(tile)
+        for m in range(BLOCKS):
+            for name, windows in (("h", h_rows), ("root", root_rows)):
+                window = keep.tile([P, S + SPARE], F32, name="%s_rows%d" % (name, m))
+                nc.gpsimd.memset(window[:, S:], 0.0)
+                windows.append(window)
 
-        warm = keep.tile([P, 1], F32, name="warm")
-        nc.scalar.activation(warm[:], h_rows[0][:, S : S + 1], ACT.Abs_reciprocal_sqrt, bias=0.5)
+        warm_up = keep.tile([P, 1], F32, name="warm_up")
+        nc.scalar.activation(warm_up[:], h_rows[0][:, S : S + 1], ACT.Abs_reciprocal_sqrt, bias=0.5)
         near_gain = keep.tile([P, PACK], F32, name="near_gain")
         nc.gpsimd.tensor_scalar(near_gain[:], gain[:], 0.75, 0.0, ALU.mult, ALU.add)
 
@@ -85,31 +91,34 @@ def tile_picked_hmixlaphopn_none_p_kernel(tc, x_words, x_scales, w1, gn, w2, w3,
         x_plane = keep.tile([P, S], U8, name="x_plane", align_bytes=64)
         nc.vector.tensor_copy(x_plane[:].bitcast(I32), picked_bytes[:].bitcast(I32))
         for r in (0, 1):
-            nc.scalar.dma_start(x_plane[2 + r : P : 32, :].bitcast(I32), x_plane[16 + r : P : 32, :].bitcast(I32))
+            nc.scalar.dma_start(
+                x_plane[2 + r : P : QUADRANT, :].bitcast(I32), x_plane[GROUP + r : P : QUADRANT, :].bitcast(I32)
+            )
+        x_codes = keep.tile([P, S], U32, name="x_codes", align_bytes=64)
+        nc.vector.tensor_copy(x_codes[:], table_words[:].indirect(offs_list[:]))
+        two_plane = keep.tile([P, S], U8, name="two_plane", tag="picked_then_two", align_bytes=64)
+        nc.vector.tensor_copy(two_plane[:], table_scales[:].indirect(two_list[:]))
         later_weights = keep.tile([P, 2, PACK, N], F32, name="later_weights", tag="scales_then_weights")
         for slot, source in enumerate((w3, w2)):
             nc.sync.dma_start(later_weights[:, slot], source.rearrange("(p j) c -> p j c", j=PACK))
-        x_codes = keep.tile([P, S], U32, name="x_codes", align_bytes=64)
-        nc.vector.tensor_copy(x_codes[:], table_words[:].indirect(offs_list[:]))
-
-        two_plane = keep.tile([P, S], U8, name="two_plane", tag="picked_then_two", align_bytes=64)
-        nc.vector.tensor_copy(two_plane[:], table_scales[:].indirect(two_list[:]))
 
         w1_rounded = keep.tile([P, PACK, P * PACK], BF16, name="w1_rounded", tag="w1_then_two", align_bytes=64)
         dealt = w1_rounded[:].rearrange("p t (m j) -> p m j t", j=PACK)
         for half, first, last, copy in (
-            (0, 0, 64, nc.scalar.copy), (1, 0, 24, nc.scalar.copy), (1, 24, 64, nc.vector.tensor_copy)
+            (0, 0, P // 2, nc.scalar.copy),
+            (1, 0, W1_SCALAR_SHARE, nc.scalar.copy),
+            (1, W1_SCALAR_SHARE, P // 2, nc.vector.tensor_copy),
         ):
             copy(
-                dealt[:, half * 64 + first : half * 64 + last],
+                dealt[:, half * P // 2 + first : half * P // 2 + last],
                 w1_raw[half][:].rearrange("p j (m t) -> p m j t", t=PACK)[:, first:last],
             )
         y_banks, y_rows = [], []
         for t in range(PACK):
-            codes, scales = quantise("w1_%d" % t, w1_rounded[:, t, :], P)
+            codes, plane = quantise("w1_%d" % t, w1_rounded[:, t, :], P)
             bank = psum.tile([P, S], F32, name="y_bank%d" % t)
             nc.tensor.matmul_mx(
-                out=bank[:], lhsT=codes[:].bitcast(FP8X4), lhsT_scale=scales[:],
+                out=bank[:], lhsT=codes[:].bitcast(FP8X4), lhsT_scale=plane[:],
                 rhs=x_codes[:].bitcast(FP8X4), rhs_scale=x_plane[:], start=True, stop=True,
             )
             y_banks.append(bank)
@@ -124,56 +133,64 @@ def tile_picked_hmixlaphopn_none_p_kernel(tc, x_words, x_scales, w1, gn, w2, w3,
         two_codes = keep.tile([P, S], U32, name="two_codes", tag="w1_then_two", align_bytes=64)
         nc.vector.tensor_copy(two_codes[:], table_words[:].indirect(two_list[:]))
 
-        def prepare_weight(name, raw):
-            rounded = keep.tile([P, N * PACK], BF16, name=name + "_rounded", tag=name + "_then_rest", align_bytes=64)
+        def prepare_weight(name, raw, tag):
+            rounded = keep.tile([P, N * PACK], BF16, name=name + "_rounded", tag=tag, align_bytes=64)
             nc.vector.tensor_copy(
-                rounded[:].rearrange("p (c i j) -> p c j i", i=4, j=PACK),
-                raw.rearrange("p j (c i) -> p c j i", i=4),
+                rounded[:].rearrange("p (c i j) -> p c j i", i=LINE, j=PACK),
+                raw.rearrange("p j (c i) -> p c j i", i=LINE),
             )
             return quantise(name, rounded[:], N)
 
-        h_banks = [psum.tile([P, S], F32, name="h_bank%d" % m) for m in range(N // P)]
+        h_banks = [psum.tile([P, S], F32, name="h_bank%d" % m) for m in range(BLOCKS)]
 
-        def second_product_pass(weight, moving_codes, moving_scales, blocks, first, last, start, stop):
-            for m in blocks:
-                block = slice(m * P, (m + 1) * P)
-                nc.tensor.matmul_mx(
-                    out=h_banks[m][:, first:last], lhsT=weight[0][:, block].bitcast(FP8X4), lhsT_scale=weight[1][:, block],
-                    rhs=moving_codes.bitcast(FP8X4), rhs_scale=moving_scales, start=start, stop=stop,
-                )
+        def h_pass(m, weight, moving_codes, moving_plane, first, last, start, stop):
+            columns = slice(m * P, (m + 1) * P)
+            nc.tensor.matmul_mx(
+                out=h_banks[m][:, first:last], lhsT=weight[0][:, columns].bitcast(FP8X4), lhsT_scale=weight[1][:, columns],
+                rhs=moving_codes.bitcast(FP8X4), rhs_scale=moving_plane, start=start, stop=stop,
+            )
 
-        def hidden_piece(first, last, tag):
+        def fetch_y(target, t, list_tile, first, last):
+            nc.scalar.activation(target[:, t, :], y_rows[t][:].indirect(entries(list_tile, first, last)), ACT.Copy)
+
+        w3_mx = prepare_weight("w3", later_weights[:, 0], "w3_rounded")
+        for m in range(1, BLOCKS):
+            h_pass(m, w3_mx, two_codes[:], two_plane[:], 0, S, True, False)
+        w2_mx = prepare_weight("w2", later_weights[:, 1], "w2_then_rest")
+        for first, last in PIECES:
             width = last - first
-            near1 = keep.tile([P, PACK, width], F32, name="near1_%d" % first)
             near2 = keep.tile([P, PACK, width], F32, name="near2_%d" % first)
-            rest = keep.tile([P, PACK, width], F32, name="rest_%d" % first, tag="w2_then_rest", align_bytes=64)
-            for t in range(PACK):
-                nc.scalar.activation(near1[:, t, :], y_rows[t][:].indirect(entries(n1_list, first, last)), ACT.Copy)
-                nc.scalar.activation(near2[:, t, :], y_rows[t][:].indirect(entries(n2_list, first, last)), ACT.Copy)
-                nc.vector.scalar_tensor_tensor(
-                    rest[:, t, :], y_banks[t][:, first:last], gain[:, t : t + 1], near1[:, t, :], ALU.mult, ALU.subtract
-                )
-            z_rounded = keep.tile([P, width * PACK], BF16, name="z_rounded%d" % first, tag=tag, align_bytes=64)
+            if first % HALF == 0:
+                base = first
+                near1 = keep.tile([P, PACK, HALF], F32, name="near1_%d" % base)
+                rest = keep.tile([P, PACK, HALF], F32, name="rest_%d" % base, tag="w2_then_rest", align_bytes=64)
+                for t in range(PACK):
+                    fetch_y(near1, t, n1_list, base, base + HALF)
+                    if width == HALF:
+                        fetch_y(near2, t, n2_list, first, last)
+                    nc.vector.scalar_tensor_tensor(
+                        rest[:, t, :], y_banks[t][:, base : base + HALF], gain[:, t : t + 1], near1[:, t, :],
+                        ALU.mult, ALU.subtract,
+                    )
+            if width < HALF:
+                for t in range(PACK):
+                    fetch_y(near2, t, n2_list, first, last)
+            z_rounded = keep.tile([P, width * PACK], BF16, name="z_rounded%d" % first, align_bytes=64)
             nc.vector.tensor_tensor(
-                z_rounded[:].rearrange("p (c i t) -> p c t i", i=4, t=PACK),
-                near2[:].rearrange("p t (c i) -> p c t i", i=4),
-                rest[:].rearrange("p t (c i) -> p c t i", i=4),
+                z_rounded[:].rearrange("p (c i t) -> p c t i", i=LINE, t=PACK),
+                near2[:].rearrange("p t (c i) -> p c t i", i=LINE),
+                rest[:, :, first - base : last - base].rearrange("p t (c i) -> p c t i", i=LINE),
                 ALU.subtract,
             )
-            return quantise("z_%d" % first, z_rounded[:], width)
-
-        w3_q = prepare_weight("w3", later_weights[:, 0])
-        second_product_pass(w3_q, two_codes[:], two_plane[:], range(1, N // P), 0, S, True, False)
-        w2_q = prepare_weight("w2", later_weights[:, 1])
-        for (first, last), tag in zip(PIECES, ("z0", "z1", "z2")):
-            z_codes, z_scales = hidden_piece(first, last, tag)
-            second_product_pass(w3_q, two_codes[:, first:last], two_plane[:, first:last], [0], first, last, True, False)
-            second_product_pass(w2_q, z_codes[:], z_scales[:], [0], first, last, False, True)
+            z_codes, z_plane = quantise("z_%d" % first, z_rounded[:], width)
+            h_pass(0, w3_mx, two_codes[:, first:last], two_plane[:, first:last], first, last, True, False)
+            h_pass(0, w2_mx, z_codes[:], z_plane[:], first, last, False, True)
             copy = nc.scalar.copy if last == S else nc.vector.tensor_copy
             copy(h_rows[0][:, first:last], h_banks[0][:, first:last])
-            second_product_pass(w2_q, z_codes[:], z_scales[:], range(1, N // P), first, last, False, last == S)
+            for m in range(1, BLOCKS):
+                h_pass(m, w2_mx, z_codes[:], z_plane[:], first, last, False, last == S)
 
-        st_rows = []
+        st_rows, size_rows = [], []
 
         def difference(m):
             if m > 0:
@@ -184,25 +201,23 @@ def tile_picked_hmixlaphopn_none_p_kernel(tc, x_words, x_scales, w1, gn, w2, w3,
             nc.vector.tensor_tensor(st[:], h_banks[m][:], other[:], ALU.subtract)
             size = keep.tile([P, S], F32, name="size%d" % m)
             nc.vector.scalar_tensor_tensor(size[:], st[:], -1.0, st[:], ALU.mult, ALU.max)
-            st_rows.append((st, size))
+            st_rows.append(st)
+            size_rows.append(size)
 
         def normalise(m):
-            st, size = st_rows[m]
-            nc.scalar.activation(root_rows[m][:, :S], size[:], ACT.Abs_reciprocal_sqrt, bias=0.5)
-            cuts = (0, 256, 384, S) if m == N // P - 1 else (0, S)
-            engine = nc.vector
-            for first, last in zip(cuts, cuts[1:]):
+            nc.scalar.activation(root_rows[m][:, :S], size_rows[m][:], ACT.Abs_reciprocal_sqrt, bias=0.5)
+            for first, last in PIECES if m == BLOCKS - 1 else ((0, S),):
                 width = last - first
                 root = keep.tile([P, width], F32, name="root%d_%d" % (m, first))
                 nc.scalar.activation(root[:], root_rows[m][:].indirect(entries(n4_list, first, last)), ACT.Copy)
-                half = keep.tile([P, width], F32, name="half%d_%d" % (m, first))
-                engine.tensor_tensor(half[:], st[:, first:last], root[:], ALU.mult)
+                once = keep.tile([P, width], F32, name="once%d_%d" % (m, first))
+                nc.vector.tensor_tensor(once[:], st_rows[m][:, first:last], root[:], ALU.mult)
                 result = keep.tile([P, width], F32, name="result%d_%d" % (m, first))
-                engine.tensor_tensor(result[:], half[:], root[:], ALU.mult)
+                nc.vector.tensor_tensor(result[:], once[:], root[:], ALU.mult)
                 nc.sync.dma_start(out[m * P : (m + 1) * P, first:last], result[:])
 
         difference(0)
-        for m in range(1, N // P):
+        for m in range(1, BLOCKS):
             difference(m)
             normalise(m - 1)
-        normalise(N // P - 1)
+        normalise(BLOCKS - 1)

from contextlib import ExitStack

import concourse.mybir as mybir

K, T, S, H, N = 512, 2048, 512, 512, 512
FLOPS = 2 * S * (K * H + H * N + K * N)

F32 = mybir.dt.float32
BF16 = mybir.dt.bfloat16
I32 = mybir.dt.int32
U32 = mybir.dt.uint32
U16 = mybir.dt.uint16
U8 = mybir.dt.uint8
FP8X4 = mybir.dt.float8_e4m3fn_x4
ALU = mybir.AluOpType
ACT = mybir.ActivationFunctionType

P = 128
PACK = 4
GROUP = 16
QUADRANT = 32
SCALE_ROWS = K // 32
LINE = 4
BLOCKS = N // P
HALF = S // 2
SPARE = 16
PIECES = ((0, HALF), (HALF, HALF + P), (HALF + P, S))
W1_SCALAR_SHARE = 24


def tile_picked_hmixlaphopn_none_p_kernel(tc, x_words, x_scales, w1, gn, w2, w3, offs, n1, n2, two, n3, n4, out):
    nc = tc.nc
    with ExitStack() as ctx:
        lists = ctx.enter_context(tc.tile_pool(name="lists", bufs=1))
        keep = ctx.enter_context(tc.tile_pool(name="keep", bufs=1))
        psum = ctx.enter_context(tc.psum_pool(name="psum", bufs=1))

        def load_list(name, source):
            tile = lists.tile([P, S // GROUP], U16, name=name)
            nc.sync.dma_start(tile[:], source)
            return tile

        def entries(list_tile, first, last):
            return list_tile[:, first // GROUP : last // GROUP]

        def quantise(name, rounded, width):
            codes = keep.tile([P, width], U32, name=name + "_codes", align_bytes=64)
            plane = keep.tile([P, width], U8, name=name + "_plane", align_bytes=64)
            nc.vector.quantize_mx(out=codes[:].bitcast(FP8X4), scales=plane[:], in_=rounded)
            return codes, plane

        table_scales = keep.tile([P, T], U8, name="table_scales", tag="scales_then_weights")
        nc.gpsimd.memset(table_scales[:].bitcast(I32), 0)
        scale_rows = x_scales[0].bitcast(I32)

        offs_list = load_list("offs_list", offs)
        two_list = load_list("two_list", two)
        table_words = keep.tile([P, T], U32, name="table_words")
        word_rows = x_words[0].rearrange("p n t -> p (n t)").bitcast(I32)
        nc.sync.dma_start(table_words[:, : T // 4].bitcast(I32), word_rows[:, : T // 4])
        for r in (0, 1):
            nc.sync.dma_start(table_scales[r:P:GROUP, :].bitcast(I32), scale_rows[r:SCALE_ROWS:2, :])
        for r in (2, 3):
            nc.sync.dma_start(table_scales[r:P:QUADRANT, :].bitcast(I32), scale_rows[r:SCALE_ROWS:4, :])
        nc.sync.dma_start(table_words[:, T // 4 :].bitcast(I32), word_rows[:, T // 4 :])
        w1_rows = w1.rearrange("(p j) c -> p j c", j=PACK)
        w1_raw = [keep.tile([P, PACK, H // 2], F32, name="w1_raw%d" % half) for half in range(2)]
        for half in range(2):
            nc.sync.dma_start(w1_raw[half][:], w1_rows[:, :, half * H // 2 : (half + 1) * H // 2])
        gain = keep.tile([P, PACK], F32, name="gain")
        nc.gpsimd.dma_start(gain[:], gn.rearrange("(p t) o -> p (t o)", t=PACK))
        n1_list = load_list("n1_list", n1)
        n2_list = load_list("n2_list", n2)
        n3_list = load_list("n3_list", n3)
        n4_list = load_list("n4_list", n4)

        h_rows, root_rows = [], []
        for m in range(BLOCKS):
            for name, windows in (("h", h_rows), ("root", root_rows)):
                window = keep.tile([P, S + SPARE], F32, name="%s_rows%d" % (name, m))
                nc.gpsimd.memset(window[:, S:], 0.0)
                windows.append(window)

        warm_up = keep.tile([P, 1], F32, name="warm_up")
        nc.scalar.activation(warm_up[:], h_rows[0][:, S : S + 1], ACT.Abs_reciprocal_sqrt, bias=0.5)
        near_gain = keep.tile([P, PACK], F32, name="near_gain")
        nc.gpsimd.tensor_scalar(near_gain[:], gain[:], 0.75, 0.0, ALU.mult, ALU.add)

        picked_bytes = keep.tile([P, S], U8, name="picked_bytes", tag="picked_then_two", align_bytes=64)
        nc.vector.tensor_copy(picked_bytes[:], table_scales[:].indirect(offs_list[:]))
        x_plane = keep.tile([P, S], U8, name="x_plane", align_bytes=64)
        nc.vector.tensor_copy(x_plane[:].bitcast(I32), picked_bytes[:].bitcast(I32))
        for r in (0, 1):
            nc.scalar.dma_start(
                x_plane[2 + r : P : QUADRANT, :].bitcast(I32), x_plane[GROUP + r : P : QUADRANT, :].bitcast(I32)
            )
        x_codes = keep.tile([P, S], U32, name="x_codes", align_bytes=64)
        nc.vector.tensor_copy(x_codes[:], table_words[:].indirect(offs_list[:]))
        two_plane = keep.tile([P, S], U8, name="two_plane", tag="picked_then_two", align_bytes=64)
        nc.vector.tensor_copy(two_plane[:], table_scales[:].indirect(two_list[:]))
        later_weights = keep.tile([P, 2, PACK, N], F32, name="later_weights", tag="scales_then_weights")
        for slot, source in enumerate((w3, w2)):
            nc.sync.dma_start(later_weights[:, slot], source.rearrange("(p j) c -> p j c", j=PACK))

        w1_rounded = keep.tile([P, PACK, P * PACK], BF16, name="w1_rounded", tag="w1_then_two", align_bytes=64)
        dealt = w1_rounded[:].rearrange("p t (m j) -> p m j t", j=PACK)
        for half, first, last, copy in (
            (0, 0, P // 2, nc.scalar.copy),
            (1, 0, W1_SCALAR_SHARE, nc.scalar.copy),
            (1, W1_SCALAR_SHARE, P // 2, nc.vector.tensor_copy),
        ):
            copy(
                dealt[:, half * P // 2 + first : half * P // 2 + last],
                w1_raw[half][:].rearrange("p j (m t) -> p m j t", t=PACK)[:, first:last],
            )
        y_banks, y_rows = [], []
        for t in range(PACK):
            codes, plane = quantise("w1_%d" % t, w1_rounded[:, t, :], P)
            bank = psum.tile([P, S], F32, name="y_bank%d" % t)
            nc.tensor.matmul_mx(
                out=bank[:], lhsT=codes[:].bitcast(FP8X4), lhsT_scale=plane[:],
                rhs=x_codes[:].bitcast(FP8X4), rhs_scale=x_plane[:], start=True, stop=True,
            )
            y_banks.append(bank)
        for t in range(PACK):
            rows = keep.tile([P, S], F32, name="y_rows%d" % t)
            if t % 2 == 0:
                nc.scalar.activation(rows[:], y_banks[t][:], ACT.Copy, scale=near_gain[:, t : t + 1])
            else:
                nc.vector.tensor_scalar(rows[:], y_banks[t][:], gain[:, t : t + 1], 0.75, ALU.mult, ALU.mult)
            y_rows.append(rows)

        two_codes = keep.tile([P, S], U32, name="two_codes", tag="w1_then_two", align_bytes=64)
        nc.vector.tensor_copy(two_codes[:], table_words[:].indirect(two_list[:]))

        def prepare_weight(name, raw, tag):
            rounded = keep.tile([P, N * PACK], BF16, name=name + "_rounded", tag=tag, align_bytes=64)
            nc.vector.tensor_copy(
                rounded[:].rearrange("p (c i j) -> p c j i", i=LINE, j=PACK),
                raw.rearrange("p j (c i) -> p c j i", i=LINE),
            )
            return quantise(name, rounded[:], N)

        h_banks = [psum.tile([P, S], F32, name="h_bank%d" % m) for m in range(BLOCKS)]

        def h_pass(m, weight, moving_codes, moving_plane, first, last, start, stop):
            columns = slice(m * P, (m + 1) * P)
            nc.tensor.matmul_mx(
                out=h_banks[m][:, first:last], lhsT=weight[0][:, columns].bitcast(FP8X4), lhsT_scale=weight[1][:, columns],
                rhs=moving_codes.bitcast(FP8X4), rhs_scale=moving_plane, start=start, stop=stop,
            )

        def fetch_y(target, t, list_tile, first, last):
            nc.scalar.activation(target[:, t, :], y_rows[t][:].indirect(entries(list_tile, first, last)), ACT.Copy)

        w3_mx = prepare_weight("w3", later_weights[:, 0], "w3_rounded")
        for m in range(1, BLOCKS):
            h_pass(m, w3_mx, two_codes[:], two_plane[:], 0, S, True, False)
        w2_mx = prepare_weight("w2", later_weights[:, 1], "w2_then_rest")
        for first, last in PIECES:
            width = last - first
            near2 = keep.tile([P, PACK, width], F32, name="near2_%d" % first)
            if first % HALF == 0:
                base = first
                near1 = keep.tile([P, PACK, HALF], F32, name="near1_%d" % base)
                rest = keep.tile([P, PACK, HALF], F32, name="rest_%d" % base, tag="w2_then_rest", align_bytes=64)
                for t in range(PACK):
                    fetch_y(near1, t, n1_list, base, base + HALF)
                    if width == HALF:
                        fetch_y(near2, t, n2_list, first, last)
                    nc.vector.scalar_tensor_tensor(
                        rest[:, t, :], y_banks[t][:, base : base + HALF], gain[:, t : t + 1], near1[:, t, :],
                        ALU.mult, ALU.subtract,
                    )
            if width < HALF:
                for t in range(PACK):
                    fetch_y(near2, t, n2_list, first, last)
            z_rounded = keep.tile([P, width * PACK], BF16, name="z_rounded%d" % first, align_bytes=64)
            nc.vector.tensor_tensor(
                z_rounded[:].rearrange("p (c i t) -> p c t i", i=LINE, t=PACK),
                near2[:].rearrange("p t (c i) -> p c t i", i=LINE),
                rest[:, :, first - base : last - base].rearrange("p t (c i) -> p c t i", i=LINE),
                ALU.subtract,
            )
            z_codes, z_plane = quantise("z_%d" % first, z_rounded[:], width)
            h_pass(0, w3_mx, two_codes[:, first:last], two_plane[:, first:last], first, last, True, False)
            h_pass(0, w2_mx, z_codes[:], z_plane[:], first, last, False, True)
            copy = nc.scalar.copy if last == S else nc.vector.tensor_copy
            copy(h_rows[0][:, first:last], h_banks[0][:, first:last])
            for m in range(1, BLOCKS):
                h_pass(m, w2_mx, z_codes[:], z_plane[:], first, last, False, last == S)

        st_rows, size_rows = [], []

        def difference(m):
            if m > 0:
                nc.vector.tensor_copy(h_rows[m][:, :S], h_banks[m][:])
            other = keep.tile([P, S], F32, name="other%d" % m)
            nc.scalar.activation(other[:], h_rows[m][:].indirect(n3_list[:]), ACT.Copy)
            st = keep.tile([P, S], F32, name="st%d" % m)
            nc.vector.tensor_tensor(st[:], h_banks[m][:], other[:], ALU.subtract)
            size = keep.tile([P, S], F32, name="size%d" % m)
            nc.vector.scalar_tensor_tensor(size[:], st[:], -1.0, st[:], ALU.mult, ALU.max)
            st_rows.append(st)
            size_rows.append(size)

        def normalise(m):
            nc.scalar.activation(root_rows[m][:, :S], size_rows[m][:], ACT.Abs_reciprocal_sqrt, bias=0.5)
            for first, last in PIECES if m == BLOCKS - 1 else ((0, S),):
                width = last - first
                root = keep.tile([P, width], F32, name="root%d_%d" % (m, first))
                nc.scalar.activation(root[:], root_rows[m][:].indirect(entries(n4_list, first, last)), ACT.Copy)
                once = keep.tile([P, width], F32, name="once%d_%d" % (m, first))
                nc.vector.tensor_tensor(once[:], st_rows[m][:, first:last], root[:], ALU.mult)
                result = keep.tile([P, width], F32, name="result%d_%d" % (m, first))
                nc.vector.tensor_tensor(result[:], once[:], root[:], ALU.mult)
                nc.sync.dma_start(out[m * P : (m + 1) * P, first:last], result[:])

        difference(0)
        for m in range(1, BLOCKS):
            difference(m)
            normalise(m - 1)
        normalise(BLOCKS - 1)
